import numpy as np, ml_dtypes
CORES = [16,32,48,64,80]
N = 5
import mx_ref
NC = 128
BF = ml_dtypes.bfloat16
def setup_inputs(rng):
    def f(*shape):
        return mx_ref.flush((rng.standard_normal(shape, dtype=np.float32) * np.exp2(rng.integers(-2, 3, shape[:-1] + (1,)))).astype(BF))
    return {"w": f(N, 128, 512), "x": f(N, 128, N * 4 * NC)}
def setup_inputs_blocks(rng):
    d = setup_inputs(rng)
    for k in ("w", "x"): d[k] = mx_ref.spread(d[k], rng, 2)
    return d
def setup_inputs_wide(rng):
    d = setup_inputs(rng)
    for k in ("w", "x"): d[k] = mx_ref.flush((d[k].astype(np.float32) * np.exp2(rng.integers(-8, 9, (N, 1, 1))).astype(np.float32)).astype(BF))
    return d
def setup_inputs_zeros(rng):
    d = setup_inputs(rng); v = d["x"].reshape(N, 128, -1, 4).copy()
    v[np.broadcast_to((rng.random((N, 1, v.shape[2], 1)) < 0.33), v.shape)] = 0
    d["x"] = v.reshape(d["x"].shape)
    return d
def reference(w, x):
    QW = [mx_ref.quantize(w[j]) for j in range(N)]
    y = np.zeros((N, 128, NC), np.float32)
    for r in range(N):
        for j in range(N):
            p = mx_ref.matmul(QW[j], mx_ref.quantize(x[j][:, 4 * NC * r:4 * NC * r + 4 * NC]))
            y[r] = p if j == 0 else y[r] + p
    return {"y": y}

@@ -1,0 +1,161 @@
+from concourse.bass import DstId, RemoteDMATransfer
+from concourse.mybir import dt
+
+N = 5
+NC = 128
+TW = 4 * NC
+
+SCRATCH = {
+    "wt": ("sbuf", [128, TW], "bfloat16"),
+    "xt": ("sbuf", [128, N * TW], "bfloat16"),
+    "wq": ("sbuf", [128, (N - 1) * NC], "float8_e4m3fn_x4"),
+    "xq": ("sbuf", [128, N * NC], "float8_e4m3fn_x4"),
+    "pl": ("sbuf", [128, (N - 1) * 2 * NC], "uint8"),
+    "po": ("sbuf", [128, NC], "uint8"),
+    "rw": ("sbuf", [128, (N - 1) * NC], "float8_e4m3fn_x4"),
+    "rx": ("sbuf", [128, (N - 1) * NC], "float8_e4m3fn_x4"),
+    "rp": ("sbuf", [128, (N - 1) * 2 * NC], "uint8"),
+    "acc": ("psum", [128, 512], "float32"),
+    "ys": ("sbuf", [128, NC], "float32"),
+}
+SEMAPHORES = ["lw", "la", "lb", "qw", "qx", "qo", "hin", "sent", "mm", "cp", "st"] + ["a%d" % s for s in range(N - 1)]
+
+
+def _bits(mask):
+    return [e for e in range(mask.bit_length()) if (mask >> e) & 1]
+
+
+def _mask(engines):
+    return sum(1 << e for e in engines)
+
+
+def _helpers(boss, T, topo):
+    free = [c for c in range(topo.CHIPS * topo.CORES_PER_CHIP)
+            if topo.chip(c) == topo.chip(boss) and c not in T.cores]
+    return ([c for c in free if topo.die(c) == topo.die(boss)], [c for c in free if topo.die(c) != topo.die(boss)])
+
+
+def _dest(j, k):
+    r = (j + 1 + k) % N
+    return r, (j if j < r else j - 1)
+
+
+def _xfer(topo, dst_core, engines, sem, src, dst):
+    rid, pid, _ = topo.addr(dst_core)
+    return RemoteDMATransfer(dst_ids=[DstId(rid=rid, pnc=pid)], dma_engine_mask=_mask(engines), remote_sem=sem,
+                             src=src, dst=dst)
+
+
+def _helper_program(g, core, boss, T, topo):
+    j = T.rank_of(boss)
+    same, other = _helpers(boss, T, topo)
+    u8 = dt.uint8
+    if core in other[:N - 1]:
+        k = other.index(core)
+        r, slot = _dest(j, k)
+        out = _bits(topo.mask(core, T.cores[r]))
+        g.wait_ge(T.sem.hin, len(_bits(topo.mask(boss, core))) // (N - 1))
+        xs = [_xfer(topo, T.cores[r], out, T.sem["a%d" % slot],
+                    T.wq[:, NC * k:NC * (k + 1)].bitcast(u8), T.rw[:, NC * slot:NC * (slot + 1)].bitcast(u8))]
+        sent = len(out)
+    elif core in same[:2]:
+        h = same.index(core)
+        g.wait_ge(T.sem.hin, len(_bits(topo.mask(boss, core))) // 4)
+        xs, sent = [], 0
+        for i in range(2):
+            k = 2 * h + i
+            r, slot = _dest(j, k)
+            out = _bits(topo.mask(core, T.cores[r]))
+            eng = out[i * len(out) // 2:(i + 1) * len(out) // 2]
+            sent += len(eng)
+            xs.append(_xfer(topo, T.cores[r], eng, T.sem["a%d" % slot],
+                            T.pl[:, 2 * NC * k:2 * NC * (k + 1)], T.rp[:, 2 * NC * slot:2 * NC * (slot + 1)]))
+    else:
+        return
+    g.remote_dma_fused(xs, local_sem=T.sem.sent)
+    g.wait_ge(T.sem.sent, sent)
+
+
+def rank_program(g, core, T, topo):
+    j = T.rank_of(core)
+    if j is None:
+        bosses = [c for c in T.cores if topo.chip(c) == topo.chip(core)]
+        if bosses:
+            _helper_program(g, core, bosses[0], T, topo)
+        return
+    u8 = dt.uint8
+    sem = T.sem
+    same, other = _helpers(core, T, topo)
+    na = N - 1 - j
+
+    g.sync.dma_start(T.wt[0:64, :], T.w[0:64, :]).then_inc(sem.lw, 16)
+    g.scalar.dma_start(T.wt[64:128, :], T.w[64:128, :]).then_inc(sem.lw, 16)
+    if na:
+        g.scalar.dma_start(T.xt[:, 0:na * TW], T.x[:, (j + 1) * TW:N * TW]).then_inc(sem.la, 16)
+    g.sync.dma_start(T.xt[:, na * TW:N * TW], T.x[:, 0:(j + 1) * TW]).then_inc(sem.lb, 16)
+
+    v = g.vector
+    v.wait_ge(sem.lw, 32)
+    for k in range(N - 1):
+        v.quantize_mx(T.wq[:, k * NC:(k + 1) * NC], T.pl[:, 2 * NC * k:2 * NC * k + NC], T.wt[:]).then_inc(sem.qw, 1)
+    for k in range(N - 1):
+        if k == 0 and na:
+            v.wait_ge(sem.la, 16)
+        if k == na:
+            v.wait_ge(sem.lb, 16)
+        v.quantize_mx(T.xq[:, k * NC:(k + 1) * NC], T.pl[:, 2 * NC * k + NC:2 * NC * (k + 1)],
+                      T.xt[:, k * TW:(k + 1) * TW]).then_inc(sem.qx, 1)
+    if na == N - 1:
+        v.wait_ge(sem.lb, 16)
+    v.quantize_mx(T.xq[:, (N - 1) * NC:N * NC], T.po[:], T.xt[:, (N - 1) * TW:N * TW]).then_inc(sem.qo, 1)
+
+    on = _bits(topo.mask(core, other[0]))
+    per = len(on) // (N - 1)
+    g.wait_ge(sem.qw, N - 1)
+    g.remote_dma_fused([_xfer(topo, other[k], on[k * per:(k + 1) * per], sem.hin,
+                              T.wq[:, k * NC:(k + 1) * NC].bitcast(u8), T.wq[:, k * NC:(k + 1) * NC].bitcast(u8))
+                        for k in range(N - 1)], local_sem=sem.sent)
+    sent = (N - 1) * per
+    xs = []
+    stay = list(on)
+    for k in range(N - 1):
+        r, slot = _dest(j, k)
+        out = _bits(topo.mask(core, T.cores[r]))
+        stay = [e for e in stay if e not in out]
+        per = len(out) // (N - 1)
+        xs.append(_xfer(topo, T.cores[r], out[k * per:(k + 1) * per], sem["a%d" % slot],
+                        T.xq[:, k * NC:(k + 1) * NC].bitcast(u8), T.rx[:, slot * NC:(slot + 1) * NC].bitcast(u8)))
+        sent += per
+    per = len(on) // 4
+    stay = stay[:2 * per]
+    for h in range(2):
+        blk = T.pl[:, 4 * NC * h:4 * NC * (h + 1)]
+        xs.append(_xfer(topo, same[h], stay[h * per:(h + 1) * per], sem.hin, blk, blk))
+        sent += per
+    g.wait_ge(sem.qx, N - 1)
+    g.remote_dma_fused(xs, local_sem=sem.sent)
+
+    t = g.tensor
+    acc = T.acc[:, 0:NC]
+    for i in range(N):
+        if i == j:
+            t.wait_ge(sem.qw, N - 1)
+            t.wait_ge(sem.qo, 1)
+            mm = t.matmul_mx(acc, T.wq[:, 0:NC], T.pl[:, 0:NC], T.xq[:, (N - 1) * NC:N * NC], T.po[:], i == 0, i == N - 1)
+        else:
+            slot = i if i < j else i - 1
+            src_same, src_other = _helpers(T.cores[i], T, topo)
+            n = (len(_bits(topo.mask(src_other[0], core))) + len(_bits(topo.mask(src_same[0], core))) // 2
+                 + len(_bits(topo.mask(T.cores[i], core))) // (N - 1))
+            t.wait_ge(sem["a%d" % slot], n)
+            mm = t.matmul_mx(acc, T.rw[:, slot * NC:(slot + 1) * NC], T.rp[:, 2 * NC * slot:2 * NC * slot + NC],
+                             T.rx[:, slot * NC:(slot + 1) * NC], T.rp[:, 2 * NC * slot + NC:2 * NC * (slot + 1)],
+                             i == 0, i == N - 1)
+    mm.then_inc(sem.mm, 1)
+
+    v.wait_ge(sem.mm, 1)
+    v.tensor_copy(T.ys[:], acc).then_inc(sem.cp, 1)
+    g.sync.wait_ge(sem.cp, 1)
+    g.sync.dma_start(T.y[:], T.ys[:]).then_inc(sem.st, 16)
+    g.sync.wait_ge(sem.st, 16)
+    g.wait_ge(sem.sent, sent)

@@ -8,9 +8,9 @@ TW = 4 * NC
 SCRATCH = {
     "wt": ("sbuf", [128, TW], "bfloat16"),
     "xt": ("sbuf", [128, N * TW], "bfloat16"),
-    "wq": ("sbuf", [128, (N - 1) * NC], "float8_e4m3fn_x4"),
+    "wq": ("sbuf", [128, 2 * NC], "float8_e4m3fn_x4"),
     "xq": ("sbuf", [128, N * NC], "float8_e4m3fn_x4"),
-    "pl": ("sbuf", [128, (N - 1) * 2 * NC], "uint8"),
+    "pl": ("sbuf", [128, 6 * NC], "uint8"),
     "po": ("sbuf", [128, NC], "uint8"),
     "rw": ("sbuf", [128, (N - 1) * NC], "float8_e4m3fn_x4"),
     "rx": ("sbuf", [128, (N - 1) * NC], "float8_e4m3fn_x4"),
@@ -18,7 +18,8 @@ SCRATCH = {
     "acc": ("psum", [128, 512], "float32"),
     "ys": ("sbuf", [128, NC], "float32"),
 }
-SEMAPHORES = ["lw", "la", "lb", "qw", "qx", "qo", "hin", "sent", "mm", "cp", "st"] + ["a%d" % s for s in range(N - 1)]
+SEMAPHORES = ["lw", "l0", "l1", "lo", "qw", "qx", "qo", "hin", "sent", "mm", "cp", "st"] + \
+             ["a%d" % s for s in range(N - 1)]
 
 
 def _bits(mask):
@@ -40,6 +41,14 @@ def _dest(j, k):
     return r, (j if j < r else j - 1)
 
 
+def _xcol(k):
+    return (3 * (k // 2) + 2 * (k % 2)) * NC
+
+
+def _wcol(k):
+    return (3 * (k // 2) + 1) * NC
+
+
 def _xfer(topo, dst_core, engines, sem, src, dst):
     rid, pid, _ = topo.addr(dst_core)
     return RemoteDMATransfer(dst_ids=[DstId(rid=rid, pnc=pid)], dma_engine_mask=_mask(engines), remote_sem=sem,
@@ -50,29 +59,31 @@ def _helper_program(g, core, boss, T, topo):
     j = T.rank_of(boss)
     same, other = _helpers(boss, T, topo)
     u8 = dt.uint8
+    sent = 0
     if core in other[:N - 1]:
         k = other.index(core)
+        c = k // 2
         r, slot = _dest(j, k)
         out = _bits(topo.mask(core, T.cores[r]))
         g.wait_ge(T.sem.hin, len(_bits(topo.mask(boss, core))) // (N - 1))
-        xs = [_xfer(topo, T.cores[r], out, T.sem["a%d" % slot],
-                    T.wq[:, NC * k:NC * (k + 1)].bitcast(u8), T.rw[:, NC * slot:NC * (slot + 1)].bitcast(u8))]
+        g.remote_dma_fused([_xfer(topo, T.cores[r], out, T.sem["a%d" % slot],
+                                  T.wq[:, NC * c:NC * (c + 1)].bitcast(u8),
+                                  T.rw[:, NC * slot:NC * (slot + 1)].bitcast(u8))], local_sem=T.sem.sent)
         sent = len(out)
     elif core in same[:2]:
         h = same.index(core)
         g.wait_ge(T.sem.hin, len(_bits(topo.mask(boss, core))) // 4)
-        xs, sent = [], 0
         for i in range(2):
             k = 2 * h + i
             r, slot = _dest(j, k)
             out = _bits(topo.mask(core, T.cores[r]))
-            eng = out[i * len(out) // 2:(i + 1) * len(out) // 2]
-            sent += len(eng)
-            xs.append(_xfer(topo, T.cores[r], eng, T.sem["a%d" % slot],
-                            T.pl[:, 2 * NC * k:2 * NC * (k + 1)], T.rp[:, 2 * NC * slot:2 * NC * (slot + 1)]))
+            lo = min(_xcol(k), _wcol(k))
+            g.remote_dma_fused([_xfer(topo, T.cores[r], out, T.sem["a%d" % slot],
+                                      T.pl[:, lo:lo + 2 * NC], T.rp[:, 2 * NC * slot:2 * NC * (slot + 1)])],
+                               local_sem=T.sem.sent)
+            sent += len(out)
     else:
         return
-    g.remote_dma_fused(xs, local_sem=T.sem.sent)
     g.wait_ge(T.sem.sent, sent)
 
 
@@ -86,34 +97,38 @@ def rank_program(g, core, T, topo):
     u8 = dt.uint8
     sem = T.sem
     same, other = _helpers(core, T, topo)
+
     na = N - 1 - j
+    pieces = [p for p in ((0, na), (na, N - 1)) if p[1] > p[0]]
+    if len(pieces) == 1:
+        pieces = [(0, (N - 1) // 2), ((N - 1) // 2, N - 1)]
+    pieces.sort(key=lambda p: p[0] - p[1])
 
     g.sync.dma_start(T.wt[0:64, :], T.w[0:64, :]).then_inc(sem.lw, 16)
     g.scalar.dma_start(T.wt[64:128, :], T.w[64:128, :]).then_inc(sem.lw, 16)
-    if na:
-        g.scalar.dma_start(T.xt[:, 0:na * TW], T.x[:, (j + 1) * TW:N * TW]).then_inc(sem.la, 16)
-    g.sync.dma_start(T.xt[:, na * TW:N * TW], T.x[:, 0:(j + 1) * TW]).then_inc(sem.lb, 16)
+    for i, (a, b) in enumerate(pieces):
+        t0 = (j + 1 + a) % N
+        g.sync.dma_start(T.xt[:, a * TW:b * TW], T.x[:, t0 * TW:(t0 + b - a) * TW]).then_inc(sem["l%d" % i], 16)
+    g.sync.dma_start(T.xt[:, (N - 1) * TW:N * TW], T.x[:, j * TW:(j + 1) * TW]).then_inc(sem.lo, 16)
 
     v = g.vector
     v.wait_ge(sem.lw, 32)
-    for k in range(N - 1):
-        v.quantize_mx(T.wq[:, k * NC:(k + 1) * NC], T.pl[:, 2 * NC * k:2 * NC * k + NC], T.wt[:]).then_inc(sem.qw, 1)
-    for k in range(N - 1):
-        if k == 0 and na:
-            v.wait_ge(sem.la, 16)
-        if k == na:
-            v.wait_ge(sem.lb, 16)
-        v.quantize_mx(T.xq[:, k * NC:(k + 1) * NC], T.pl[:, 2 * NC * k + NC:2 * NC * (k + 1)],
-                      T.xt[:, k * TW:(k + 1) * TW]).then_inc(sem.qx, 1)
-    if na == N - 1:
-        v.wait_ge(sem.lb, 16)
+    for c in range(2):
+        v.quantize_mx(T.wq[:, c * NC:(c + 1) * NC], T.pl[:, _wcol(2 * c):_wcol(2 * c) + NC], T.wt[:]).then_inc(sem.qw, 1)
+    for i, (a, b) in enumerate(pieces):
+        v.wait_ge(sem["l%d" % i], 16)
+        for k in range(a, b):
+            v.quantize_mx(T.xq[:, k * NC:(k + 1) * NC], T.pl[:, _xcol(k):_xcol(k) + NC],
+                          T.xt[:, k * TW:(k + 1) * TW]).then_inc(sem.qx, 1)
+    v.wait_ge(sem.lo, 16)
     v.quantize_mx(T.xq[:, (N - 1) * NC:N * NC], T.po[:], T.xt[:, (N - 1) * TW:N * TW]).then_inc(sem.qo, 1)
 
     on = _bits(topo.mask(core, other[0]))
     per = len(on) // (N - 1)
-    g.wait_ge(sem.qw, N - 1)
+    g.wait_ge(sem.qw, 2)
     g.remote_dma_fused([_xfer(topo, other[k], on[k * per:(k + 1) * per], sem.hin,
-                              T.wq[:, k * NC:(k + 1) * NC].bitcast(u8), T.wq[:, k * NC:(k + 1) * NC].bitcast(u8))
+                              T.wq[:, (k // 2) * NC:(k // 2 + 1) * NC].bitcast(u8),
+                              T.wq[:, (k // 2) * NC:(k // 2 + 1) * NC].bitcast(u8))
                         for k in range(N - 1)], local_sem=sem.sent)
     sent = (N - 1) * per
     xs = []
@@ -129,7 +144,7 @@ def rank_program(g, core, T, topo):
     per = len(on) // 4
     stay = stay[:2 * per]
     for h in range(2):
-        blk = T.pl[:, 4 * NC * h:4 * NC * (h + 1)]
+        blk = T.pl[:, 2 * NC * h:2 * NC * h + 4 * NC]
         xs.append(_xfer(topo, same[h], stay[h * per:(h + 1) * per], sem.hin, blk, blk))
         sent += per
     g.wait_ge(sem.qx, N - 1)
@@ -137,20 +152,23 @@ def rank_program(g, core, T, topo):
 
     t = g.tensor
     acc = T.acc[:, 0:NC]
-    for i in range(N):
-        if i == j:
-            t.wait_ge(sem.qw, N - 1)
-            t.wait_ge(sem.qo, 1)
-            mm = t.matmul_mx(acc, T.wq[:, 0:NC], T.pl[:, 0:NC], T.xq[:, (N - 1) * NC:N * NC], T.po[:], i == 0, i == N - 1)
-        else:
-            slot = i if i < j else i - 1
-            src_same, src_other = _helpers(T.cores[i], T, topo)
-            n = (len(_bits(topo.mask(src_other[0], core))) + len(_bits(topo.mask(src_same[0], core))) // 2
-                 + len(_bits(topo.mask(T.cores[i], core))) // (N - 1))
-            t.wait_ge(sem["a%d" % slot], n)
-            mm = t.matmul_mx(acc, T.rw[:, slot * NC:(slot + 1) * NC], T.rp[:, 2 * NC * slot:2 * NC * slot + NC],
-                             T.rx[:, slot * NC:(slot + 1) * NC], T.rp[:, 2 * NC * slot + NC:2 * NC * (slot + 1)],
-                             i == 0, i == N - 1)
+    t.wait_ge(sem.qw, 2)
+    t.wait_ge(sem.qo, 1)
+    t.matmul_mx(acc, T.wq[:, 0:NC], T.pl[:, _wcol(0):_wcol(0) + NC], T.xq[:, (N - 1) * NC:N * NC], T.po[:], True, False)
+    senders = sorted((i for i in range(N) if i != j), key=lambda i: (((j - i - 1) % N) % 2, (j - i - 1) % N))
+    for n_done, i in enumerate(senders):
+        k = (j - i - 1) % N
+        slot = i if i < j else i - 1
+        src_same, src_other = _helpers(T.cores[i], T, topo)
+        n = (len(_bits(topo.mask(src_other[0], core))) + len(_bits(topo.mask(src_same[0], core)))
+             + len(_bits(topo.mask(T.cores[i], core))) // (N - 1))
+        lo = min(_xcol(k), _wcol(k))
+        pw = 2 * NC * slot + _wcol(k) - lo
+        px = 2 * NC * slot + _xcol(k) - lo
+        t.wait_ge(sem["a%d" % slot], n)
+        mm = t.matmul_mx(acc, T.rw[:, slot * NC:(slot + 1) * NC], T.rp[:, pw:pw + NC],
+                         T.rx[:, slot * NC:(slot + 1) * NC], T.rp[:, px:px + NC],
+                         False, n_done == N - 2)
     mm.then_inc(sem.mm, 1)
 
     v.wait_ge(sem.mm, 1)

from concourse.bass import DstId, RemoteDMATransfer
from concourse.mybir import dt

N = 5
NC = 128
TW = 4 * NC

SCRATCH = {
    "wt": ("sbuf", [128, TW], "bfloat16"),
    "xt": ("sbuf", [128, N * TW], "bfloat16"),
    "wq": ("sbuf", [128, 2 * NC], "float8_e4m3fn_x4"),
    "xq": ("sbuf", [128, N * NC], "float8_e4m3fn_x4"),
    "pl": ("sbuf", [128, 6 * NC], "uint8"),
    "po": ("sbuf", [128, NC], "uint8"),
    "rw": ("sbuf", [128, (N - 1) * NC], "float8_e4m3fn_x4"),
    "rx": ("sbuf", [128, (N - 1) * NC], "float8_e4m3fn_x4"),
    "rp": ("sbuf", [128, (N - 1) * 2 * NC], "uint8"),
    "acc": ("psum", [128, 512], "float32"),
    "ys": ("sbuf", [128, NC], "float32"),
}
SEMAPHORES = ["lw", "l0", "l1", "lo", "qw", "qx", "qo", "hin", "sent", "mm", "cp", "st"] + \
             ["a%d" % s for s in range(N - 1)]


def _bits(mask):
    return [e for e in range(mask.bit_length()) if (mask >> e) & 1]


def _mask(engines):
    return sum(1 << e for e in engines)


def _helpers(boss, T, topo):
    free = [c for c in range(topo.CHIPS * topo.CORES_PER_CHIP)
            if topo.chip(c) == topo.chip(boss) and c not in T.cores]
    return ([c for c in free if topo.die(c) == topo.die(boss)], [c for c in free if topo.die(c) != topo.die(boss)])


def _dest(j, k):
    r = (j + 1 + k) % N
    return r, (j if j < r else j - 1)


def _xcol(k):
    return (3 * (k // 2) + 2 * (k % 2)) * NC


def _wcol(k):
    return (3 * (k // 2) + 1) * NC


def _xfer(topo, dst_core, engines, sem, src, dst):
    rid, pid, _ = topo.addr(dst_core)
    return RemoteDMATransfer(dst_ids=[DstId(rid=rid, pnc=pid)], dma_engine_mask=_mask(engines), remote_sem=sem,
                             src=src, dst=dst)


def _helper_program(g, core, boss, T, topo):
    j = T.rank_of(boss)
    same, other = _helpers(boss, T, topo)
    u8 = dt.uint8
    sent = 0
    if core in other[:N - 1]:
        k = other.index(core)
        c = k // 2
        r, slot = _dest(j, k)
        out = _bits(topo.mask(core, T.cores[r]))
        g.wait_ge(T.sem.hin, len(_bits(topo.mask(boss, core))) // (N - 1))
        g.remote_dma_fused([_xfer(topo, T.cores[r], out, T.sem["a%d" % slot],
                                  T.wq[:, NC * c:NC * (c + 1)].bitcast(u8),
                                  T.rw[:, NC * slot:NC * (slot + 1)].bitcast(u8))], local_sem=T.sem.sent)
        sent = len(out)
    elif core in same[:2]:
        h = same.index(core)
        g.wait_ge(T.sem.hin, len(_bits(topo.mask(boss, core))) // 4)
        for i in range(2):
            k = 2 * h + i
            r, slot = _dest(j, k)
            out = _bits(topo.mask(core, T.cores[r]))
            lo = min(_xcol(k), _wcol(k))
            g.remote_dma_fused([_xfer(topo, T.cores[r], out, T.sem["a%d" % slot],
                                      T.pl[:, lo:lo + 2 * NC], T.rp[:, 2 * NC * slot:2 * NC * (slot + 1)])],
                               local_sem=T.sem.sent)
            sent += len(out)
    else:
        return
    g.wait_ge(T.sem.sent, sent)


def rank_program(g, core, T, topo):
    j = T.rank_of(core)
    if j is None:
        bosses = [c for c in T.cores if topo.chip(c) == topo.chip(core)]
        if bosses:
            _helper_program(g, core, bosses[0], T, topo)
        return
    u8 = dt.uint8
    sem = T.sem
    same, other = _helpers(core, T, topo)

    na = N - 1 - j
    pieces = [p for p in ((0, na), (na, N - 1)) if p[1] > p[0]]
    if len(pieces) == 1:
        pieces = [(0, (N - 1) // 2), ((N - 1) // 2, N - 1)]
    pieces.sort(key=lambda p: p[0] - p[1])

    g.sync.dma_start(T.wt[0:64, :], T.w[0:64, :]).then_inc(sem.lw, 16)
    g.scalar.dma_start(T.wt[64:128, :], T.w[64:128, :]).then_inc(sem.lw, 16)
    for i, (a, b) in enumerate(pieces):
        t0 = (j + 1 + a) % N
        g.sync.dma_start(T.xt[:, a * TW:b * TW], T.x[:, t0 * TW:(t0 + b - a) * TW]).then_inc(sem["l%d" % i], 16)
    g.sync.dma_start(T.xt[:, (N - 1) * TW:N * TW], T.x[:, j * TW:(j + 1) * TW]).then_inc(sem.lo, 16)

    v = g.vector
    v.wait_ge(sem.lw, 32)
    for c in range(2):
        v.quantize_mx(T.wq[:, c * NC:(c + 1) * NC], T.pl[:, _wcol(2 * c):_wcol(2 * c) + NC], T.wt[:]).then_inc(sem.qw, 1)
    for i, (a, b) in enumerate(pieces):
        v.wait_ge(sem["l%d" % i], 16)
        for k in range(a, b):
            v.quantize_mx(T.xq[:, k * NC:(k + 1) * NC], T.pl[:, _xcol(k):_xcol(k) + NC],
                          T.xt[:, k * TW:(k + 1) * TW]).then_inc(sem.qx, 1)
    v.wait_ge(sem.lo, 16)
    v.quantize_mx(T.xq[:, (N - 1) * NC:N * NC], T.po[:], T.xt[:, (N - 1) * TW:N * TW]).then_inc(sem.qo, 1)

    on = _bits(topo.mask(core, other[0]))
    per = len(on) // (N - 1)
    g.wait_ge(sem.qw, 2)
    g.remote_dma_fused([_xfer(topo, other[k], on[k * per:(k + 1) * per], sem.hin,
                              T.wq[:, (k // 2) * NC:(k // 2 + 1) * NC].bitcast(u8),
                              T.wq[:, (k // 2) * NC:(k // 2 + 1) * NC].bitcast(u8))
                        for k in range(N - 1)], local_sem=sem.sent)
    sent = (N - 1) * per
    xs = []
    stay = list(on)
    for k in range(N - 1):
        r, slot = _dest(j, k)
        out = _bits(topo.mask(core, T.cores[r]))
        stay = [e for e in stay if e not in out]
        per = len(out) // (N - 1)
        xs.append(_xfer(topo, T.cores[r], out[k * per:(k + 1) * per], sem["a%d" % slot],
                        T.xq[:, k * NC:(k + 1) * NC].bitcast(u8), T.rx[:, slot * NC:(slot + 1) * NC].bitcast(u8)))
        sent += per
    per = len(on) // 4
    stay = stay[:2 * per]
    for h in range(2):
        blk = T.pl[:, 2 * NC * h:2 * NC * h + 4 * NC]
        xs.append(_xfer(topo, same[h], stay[h * per:(h + 1) * per], sem.hin, blk, blk))
        sent += per
    g.wait_ge(sem.qx, N - 1)
    g.remote_dma_fused(xs, local_sem=sem.sent)

    t = g.tensor
    acc = T.acc[:, 0:NC]
    t.wait_ge(sem.qw, 2)
    t.wait_ge(sem.qo, 1)
    t.matmul_mx(acc, T.wq[:, 0:NC], T.pl[:, _wcol(0):_wcol(0) + NC], T.xq[:, (N - 1) * NC:N * NC], T.po[:], True, False)
    senders = sorted((i for i in range(N) if i != j), key=lambda i: (((j - i - 1) % N) % 2, (j - i - 1) % N))
    for n_done, i in enumerate(senders):
        k = (j - i - 1) % N
        slot = i if i < j else i - 1
        src_same, src_other = _helpers(T.cores[i], T, topo)
        n = (len(_bits(topo.mask(src_other[0], core))) + len(_bits(topo.mask(src_same[0], core)))
             + len(_bits(topo.mask(T.cores[i], core))) // (N - 1))
        lo = min(_xcol(k), _wcol(k))
        pw = 2 * NC * slot + _wcol(k) - lo
        px = 2 * NC * slot + _xcol(k) - lo
        t.wait_ge(sem["a%d" % slot], n)
        mm = t.matmul_mx(acc, T.rw[:, slot * NC:(slot + 1) * NC], T.rp[:, pw:pw + NC],
                         T.rx[:, slot * NC:(slot + 1) * NC], T.rp[:, px:px + NC],
                         False, n_done == N - 2)
    mm.then_inc(sem.mm, 1)

    v.wait_ge(sem.mm, 1)
    v.tensor_copy(T.ys[:], acc).then_inc(sem.cp, 1)
    g.sync.wait_ge(sem.cp, 1)
    g.sync.dma_start(T.y[:], T.ys[:]).then_inc(sem.st, 16)
    g.sync.wait_ge(sem.st, 16)
    g.wait_ge(sem.sent, sent)
